import numpy as np
import ml_dtypes


def mxq(x, axis, fmt="e4m3"):
    dtype, down = {"e4m3": (ml_dtypes.float8_e4m3fn, 7), "e5m2": (ml_dtypes.float8_e5m2, 14)}[fmt]
    v = np.moveaxis(np.asarray(x, np.float32).astype(ml_dtypes.bfloat16).astype(np.float64), axis, -1)
    blocks = v.reshape(v.shape[:-1] + (-1, 32))
    amax = np.abs(blocks).max(-1, keepdims=True)
    byte = np.maximum(np.where(amax > 0, np.frexp(amax)[1] - 1 + 127, 0) - down, 1)
    scale = np.exp2(byte - 127.0)
    codes = (blocks / scale).astype(np.float32).astype(dtype).astype(np.float64)
    return np.moveaxis((codes * scale).reshape(v.shape), -1, axis)


WIDE = False


def mx_kscale(k):
    if not WIDE:
        return np.ones(k)
    levels = np.array([10, -10, 5, -5, 0])
    if k % 512:
        return np.exp2(np.random.permutation(np.resize(levels, k // 32))).repeat(32)
    a = np.empty((k // 512, 16))
    for p in range(k // 512):
        a[p, :8] = np.random.permutation(np.resize(levels, 8))
        for g in range(8):
            far = levels[np.abs(levels - a[p, g]) >= 10]
            a[p, g + 8] = far[np.random.randint(len(far))]
    return np.exp2(a.ravel()).repeat(32)


def f64(x):
    return np.asarray(x).astype(np.float64)


def striped8(idx):
    return np.asarray(idx).reshape(8, -1, 16).transpose(0, 2, 1).reshape(128, -1).astype(np.uint16)


def unstriped8(offs):
    return offs.reshape(8, 16, -1).transpose(0, 2, 1).reshape(8, -1).astype(np.int64)


def pick8(x, idx, run):
    r = np.arange(len(x))
    return x[r[:, None], idx[r % (8 * run) // run]]


E2M1 = np.array([0.0, 0.5, 1.0, 1.5, 2.0, 3.0, 4.0, 6.0, -0.0, -0.5, -1.0, -1.5, -2.0, -3.0, -4.0, -6.0])


def pack_weight(w, fmt):
    k, n = w.shape
    w = f64(np.asarray(w, np.float32).astype(ml_dtypes.bfloat16)).reshape(k // 32, 32, n)
    amax = np.abs(w).max(1)
    if fmt == "e4m3":
        byte = np.frexp(amax)[1] - 1 + 127 - 7
    else:
        mant, ex = np.frexp(amax / 6.0)
        byte = np.where(mant > 0.5, ex, ex - 1) + 127
    byte = np.clip(np.where(amax > 0, byte, 1), 1, 254)
    scaled = (w * np.exp2(127.0 - byte)[:, None, :]).reshape(k, n).astype(np.float32)
    by_word = np.ascontiguousarray(scaled.reshape(k // 512, 128, 4, n).transpose(0, 1, 3, 2))
    if fmt == "e4m3":
        words = by_word.astype(ml_dtypes.float8_e4m3fn).view(np.uint8)
    else:
        c = by_word.astype(ml_dtypes.float4_e2m1fn).view(np.uint8) & 0xF
        words = (c[..., 0::2] | (c[..., 1::2] << 4)).reshape(k // 512, 128, 2 * n)
    return np.ascontiguousarray(words), np.ascontiguousarray(byte.astype(np.uint8).reshape(k // 512, 16, n))


def unpack_weight(words, scales, fmt):
    g, _, n = scales.shape
    words = np.ascontiguousarray(words).reshape(g, 128, n, -1)
    if fmt == "e4m3":
        vals = words.view(ml_dtypes.float8_e4m3fn).astype(np.float64)
    else:
        nib = np.empty((g, 128, n, 4), np.uint8)
        nib[..., 0::2] = words & 0xF
        nib[..., 1::2] = words >> 4
        vals = E2M1[nib]
    vals = vals * np.repeat(np.exp2(scales.astype(np.float64) - 127.0), 8, axis=1)[..., None]
    return vals.transpose(0, 1, 3, 2).reshape(g * 512, n)


def sigmoid(v):
    return 1.0 / (1.0 + np.exp(-v))


def bf(x):
    return np.asarray(x, np.float32).astype(ml_dtypes.bfloat16)


def planes(Y):
    r, m = Y.shape
    b = f64(bf(Y)).reshape(r // 32, 32, m)
    amax = np.abs(b).max(1)
    byte = np.clip(np.where(amax > 0, np.frexp(amax)[1] - 1 + 127 - 7, 1), 1, 254)
    codes = (b * np.exp2(127.0 - byte)[:, None, :]).reshape(r, m).astype(np.float32).astype(ml_dtypes.float8_e4m3fn).view(np.uint8)
    words = codes.reshape(r // 512, 128, 4, m).transpose(0, 1, 3, 2)
    return np.ascontiguousarray(words), np.ascontiguousarray(byte.astype(np.uint8).reshape(r // 512, 16, m))


K, T, J, N, L = 512, 1024, 256, 512, 512


def setup_inputs():
    n = np.random.standard_normal
    idx = np.stack([np.random.permutation(T)[:J] for _ in range(8)])
    fk = mx_kscale(K)
    fl = mx_kscale(L)
    wvp = pack_weight(n((K, N)) * 1 / np.sqrt(K) * fk[:, None], "e2m1")
    xgp = pack_weight(n((L, J)) / fl[:, None], "e4m3")
    wgp = pack_weight(n((L, N)) * 1 / np.sqrt(L) * fl[:, None], "e2m1")
    return {
        "xv": (n((K, J)) / fk[:, None]).astype(np.float32),
        "wv_words": wvp[0],
        "wv_scales": wvp[1],
        "xg_words": xgp[0],
        "xg_scales": xgp[1],
        "wg_words": wgp[0],
        "wg_scales": wgp[1],
        "old": (1.0 * n((N, T))).astype(np.float32),
        "offs": striped8(idx),
    }


def reference(xv, wv_words, wv_scales, xg_words, xg_scales, wg_words, wg_scales, old, offs):
    idx = unstriped8(offs)
    wvu = unpack_weight(wv_words, wv_scales, "e2m1")
    xgu = unpack_weight(xg_words, xg_scales, "e4m3")
    wgu = unpack_weight(wg_words, wg_scales, "e2m1")
    xvq = mxq(f64(xv), 0, "e4m3")
    v = wvu.T @ xvq
    g = wgu.T @ xgu
    d = sigmoid(g) * (v - pick8(f64(old), idx, 64))
    p = np.zeros((N, T))
    p[np.arange(N)[:, None], idx[np.arange(N) % 512 // 64]] = d
    y = f64(old) + p
    words, scales = planes(y)
    return y, words, scales

@@ -1,0 +1,183 @@
+from contextlib import ExitStack
+
+import concourse.mybir as mybir
+from concourse.masks import make_identity
+
+K, T, J, N, L = 512, 1024, 256, 512, 512
+FLOPS = 2 * K * N * J + 2 * L * N * J
+
+F32 = mybir.dt.float32
+BF16 = mybir.dt.bfloat16
+I32 = mybir.dt.int32
+U32 = mybir.dt.uint32
+U16 = mybir.dt.uint16
+U8 = mybir.dt.uint8
+E4M3 = mybir.dt.float8_e4m3fn_x4
+E2M1 = mybir.dt.float4_e2m1fn_x4
+ALU = mybir.AluOpType
+ACT = mybir.ActivationFunctionType
+
+P = 128
+PACK = 4
+CHUNK = 256
+N_CHUNKS = T // CHUNK
+
+
+def tile_list_head_page_drift_pl_kernel(
+    tc, xv, wv_words, wv_scales, xg_words, xg_scales, wg_words, wg_scales, old, offs, out_0, out_1, out_2
+):
+    nc = tc.nc
+    old_rows = old.rearrange("(p t) c -> t p c", t=PACK)
+    out_rows = out_0.rearrange("(p t) c -> t p c", t=PACK)
+
+    with ExitStack() as ctx:
+        keep = ctx.enter_context(tc.tile_pool(name="keep", bufs=1))
+        psum = ctx.enter_context(tc.psum_pool(name="psum", bufs=1))
+
+        offsets = keep.tile([P, J // 16], U16, name="offsets")
+
+        WG0, XG0, WV0, SCALE_BYTES = 0, N, N + J, 2 * N + J
+        staged = keep.tile([16, SCALE_BYTES], U8, name="staged", tag="late3")
+        nc.sync.dma_start(staged[:, WG0:XG0].bitcast(I32), wg_scales[0].bitcast(I32))
+        nc.sync.dma_start(staged[:, XG0:WV0].bitcast(I32), xg_scales[0].bitcast(I32))
+        nc.sync.dma_start(staged[:, WV0:SCALE_BYTES].bitcast(I32), wv_scales[0].bitcast(I32))
+        nc.sync.dma_start(offsets[:], offs)
+        wv_raw = keep.tile([P, 2 * N], U8, name="wv_raw", tag="late1")
+        nc.sync.dma_start(wv_raw[:].bitcast(I32), wv_words[0].bitcast(I32))
+        xv_raw = keep.tile([P, PACK, J], F32, name="xv_raw", tag="late2")
+        nc.sync.dma_start(xv_raw[:], xv.rearrange("(p t) j -> p t j", t=PACK))
+        xg_codes = keep.tile([P, J], U32, name="xg_codes", align_bytes=64)
+        nc.sync.dma_start(xg_codes[:].bitcast(I32), xg_words[0].rearrange("p j t -> p (j t)").bitcast(I32))
+        wg_codes = keep.tile([P, 2 * N], U8, name="wg_codes", align_bytes=64)
+        nc.sync.dma_start(wg_codes[:].bitcast(I32), wg_words[0].bitcast(I32))
+        old_sb = [keep.tile([P, T], F32, name="old0")]
+        nc.sync.dma_start(old_sb[0][:], old_rows[0])
+
+        in_scales = keep.tile([P, SCALE_BYTES], U8, name="in_scales", align_bytes=64)
+        nc.vector.memset(in_scales[:].bitcast(I32), 0)
+        for q in range(4):
+            nc.scalar.dma_start(
+                in_scales[32 * q : 32 * q + 4, :].bitcast(I32), staged[4 * q : 4 * q + 4, :].bitcast(I32)
+            )
+
+        pages = [keep.tile([P, T], F32, name="page%d" % i) for i in range(PACK)]
+        for page in pages:
+            nc.vector.memset(page[:], 0.0)
+        identity = keep.tile([P, P], F32, name="identity")
+        make_identity(nc, identity[:])
+
+        wv_codes = keep.tile([P, 2 * N], U8, name="wv_codes", align_bytes=64)
+        nc.vector.tensor_copy(
+            wv_codes[:].bitcast(U16).rearrange("p (t q) -> p t q", t=PACK),
+            wv_raw[:].bitcast(U16).rearrange("p (q t) -> p t q", t=PACK),
+        )
+
+        xv_bf = keep.tile([P, J, PACK], BF16, name="xv_bf", align_bytes=64)
+        nc.vector.tensor_copy(
+            xv_bf[:].rearrange("p (c i) t -> p c t i", i=4), xv_raw[:].rearrange("p t (c i) -> p c t i", i=4)
+        )
+        xv_codes = keep.tile([P, J], U32, name="xv_codes", align_bytes=64)
+        xv_scale = keep.tile([P, J], U8, name="xv_scale", align_bytes=64)
+        nc.vector.quantize_mx(
+            out=xv_codes[:].bitcast(E4M3), scales=xv_scale[:], in_=xv_bf[:].rearrange("p j t -> p (j t)")
+        )
+        wv_scale = keep.tile([P, N], U8, name="wv_scale", align_bytes=64)
+        nc.vector.tensor_copy(
+            wv_scale[:].rearrange("p (t q) -> p t q", t=PACK),
+            in_scales[:, WV0:SCALE_BYTES].rearrange("p (q t) -> p t q", t=PACK),
+        )
+
+        for t in range(1, PACK):
+            old_t = keep.tile([P, T], F32, name="old%d" % t, tag="late%d" % t)
+            nc.sync.dma_start(old_t[:], old_rows[t])
+            old_sb.append(old_t)
+
+        g_ps = []
+        for h in range(2):
+            bank = psum.tile([P, N], F32, name="g_ps%d" % h)
+            nc.tensor.matmul_mx(
+                out=bank[:],
+                lhsT=xg_codes[:, h * P : (h + 1) * P].bitcast(E4M3),
+                lhsT_scale=in_scales[:, XG0 + h * P : XG0 + (h + 1) * P],
+                rhs=wg_codes[:].bitcast(E2M1),
+                rhs_scale=in_scales[:, WG0:XG0],
+                start=True,
+                stop=True,
+            )
+            g_ps.append(bank)
+
+        v_ps = []
+        gate_ps = []
+        for u in range(2):
+            v_bank = psum.tile([P, 2, J], F32, name="v_ps%d" % u)
+            for e in range(2):
+                t = 2 * u + e
+                nc.tensor.matmul_mx(
+                    out=v_bank[:, e, :],
+                    lhsT=wv_codes[:, 2 * P * t : 2 * P * (t + 1)].bitcast(E2M1),
+                    lhsT_scale=wv_scale[:, P * t : P * (t + 1)],
+                    rhs=xv_codes[:].bitcast(E4M3),
+                    rhs_scale=xv_scale[:],
+                    start=True,
+                    stop=True,
+                )
+            v_ps.append(v_bank)
+            gate_bank = psum.tile([P, 2, J], F32, name="gate_ps%d" % u)
+            for h in range(2):
+                gate_t = keep.tile([P, 2, P], F32, name="gate_t%d%d" % (u, h))
+                nc.scalar.activation(
+                    gate_t[:], g_ps[h][:].rearrange("j (q t) -> j t q", t=PACK)[:, 2 * u : 2 * u + 2, :], ACT.Sigmoid
+                )
+                for e in range(2):
+                    nc.tensor.transpose(gate_bank[:, e, h * P : (h + 1) * P], gate_t[:, e, :], identity[:])
+            gate_ps.append(gate_bank)
+
+        y = [keep.tile([P, 2, T], F32, name="y%d" % u) for u in range(2)]
+        y_bf = [keep.tile([P, CHUNK, PACK], BF16, name="y_bf%d" % c, align_bytes=64) for c in range(N_CHUNKS)]
+
+        def round_pair(engine_copy, u, c):
+            cols = slice(c * CHUNK, (c + 1) * CHUNK)
+            engine_copy(
+                y_bf[c][:, :, 2 * u : 2 * u + 2].rearrange("p (c i) t -> p c t i", i=4),
+                y[u][:, :, cols].rearrange("p t (c i) -> p c t i", i=4),
+            )
+
+        for t in range(PACK):
+            u, e = divmod(t, 2)
+            picked = keep.tile([P, J], F32, name="picked%d" % t)
+            nc.scalar.activation(picked[:], old_sb[t][:].indirect(offsets[:]), ACT.Copy)
+            diff = keep.tile([P, J], F32, name="diff%d" % t)
+            nc.vector.tensor_tensor(diff[:], v_ps[u][:, e, :], picked[:], ALU.subtract)
+            drift = keep.tile([P, J], F32, name="drift%d" % t)
+            nc.vector.tensor_tensor(drift[:], gate_ps[u][:, e, :], diff[:], ALU.mult)
+            page = pages[t]
+            nc.vector.tensor_copy(page[:].indirect(offsets[:]), drift[:])
+            if t < PACK - 1:
+                nc.gpsimd.tensor_tensor(y[u][:, e, :], old_sb[t][:], page[:], ALU.add)
+                nc.sync.dma_start(out_rows[t], y[u][:, e, :])
+            if t == 1:
+                for c in range(N_CHUNKS):
+                    round_pair(nc.scalar.copy, 0, c)
+
+        y_scale = keep.tile([P, T], U8, name="y_scale", align_bytes=64)
+        last = PACK - 1
+        for c in range(N_CHUNKS):
+            cols = slice(c * CHUNK, (c + 1) * CHUNK)
+            nc.vector.tensor_tensor(y[1][:, 1, cols], old_sb[last][:, cols], pages[last][:, cols], ALU.add)
+            if c % 2 == 1:
+                half = slice((c - 1) * CHUNK, (c + 1) * CHUNK)
+                nc.sync.dma_start(out_rows[last][:, half], y[1][:, 1, half])
+        words_out = out_1[0].rearrange("p c t -> p (c t)").bitcast(I32)
+        for c in (0, 3, 1, 2):
+            cols = slice(c * CHUNK, (c + 1) * CHUNK)
+            round_pair(nc.vector.tensor_copy if c == 3 else nc.scalar.copy, 1, c)
+            y_codes = keep.tile([P, CHUNK], U32, name="y_codes%d" % c, align_bytes=64)
+            nc.vector.quantize_mx(
+                out=y_codes[:].bitcast(E4M3), scales=y_scale[:, cols], in_=y_bf[c][:].rearrange("p c t -> p (c t)")
+            )
+            nc.sync.dma_start(words_out[:, cols], y_codes[:].bitcast(I32))
+        for q in range(4):
+            queue = nc.sync if q % 2 else nc.scalar
+            queue.dma_start(
+                out_2[0, 4 * q : 4 * q + 4, :].bitcast(I32), y_scale[32 * q : 32 * q + 4, :].bitcast(I32)
+            )

@@ -19,6 +19,7 @@ ACT = mybir.ActivationFunctionType
 
 P = 128
 PACK = 4
+BANK = 512
 CHUNK = 256
 N_CHUNKS = T // CHUNK
 
@@ -27,8 +28,8 @@ def tile_list_head_page_drift_pl_kernel(
     tc, xv, wv_words, wv_scales, xg_words, xg_scales, wg_words, wg_scales, old, offs, out_0, out_1, out_2
 ):
     nc = tc.nc
-    old_rows = old.rearrange("(p t) c -> t p c", t=PACK)
-    out_rows = out_0.rearrange("(p t) c -> t p c", t=PACK)
+    old_rows = old.rearrange("(p t) c -> p t c", t=PACK)
+    out_rows = out_0.rearrange("(p t) c -> p t c", t=PACK)
 
     with ExitStack() as ctx:
         keep = ctx.enter_context(tc.tile_pool(name="keep", bufs=1))
@@ -36,22 +37,22 @@ def tile_list_head_page_drift_pl_kernel(
 
         offsets = keep.tile([P, J // 16], U16, name="offsets")
 
-        WG0, XG0, WV0, SCALE_BYTES = 0, N, N + J, 2 * N + J
-        staged = keep.tile([16, SCALE_BYTES], U8, name="staged", tag="late3")
-        nc.sync.dma_start(staged[:, WG0:XG0].bitcast(I32), wg_scales[0].bitcast(I32))
-        nc.sync.dma_start(staged[:, XG0:WV0].bitcast(I32), xg_scales[0].bitcast(I32))
-        nc.sync.dma_start(staged[:, WV0:SCALE_BYTES].bitcast(I32), wv_scales[0].bitcast(I32))
+        WG0, WV0, XG0, SCALE_BYTES = 0, N, 2 * N, 2 * N + J
+        staged = keep.tile([16, SCALE_BYTES], U8, name="staged", tag="pick0", align_bytes=64)
+        nc.sync.dma_start(staged[:, WG0:WV0].bitcast(I32), wg_scales[0].bitcast(I32))
+        nc.sync.dma_start(staged[:, WV0:XG0].bitcast(I32), wv_scales[0].bitcast(I32))
+        nc.sync.dma_start(staged[:, XG0:SCALE_BYTES].bitcast(I32), xg_scales[0].bitcast(I32))
         nc.sync.dma_start(offsets[:], offs)
         wv_raw = keep.tile([P, 2 * N], U8, name="wv_raw", tag="late1")
         nc.sync.dma_start(wv_raw[:].bitcast(I32), wv_words[0].bitcast(I32))
         xv_raw = keep.tile([P, PACK, J], F32, name="xv_raw", tag="late2")
         nc.sync.dma_start(xv_raw[:], xv.rearrange("(p t) j -> p t j", t=PACK))
-        xg_codes = keep.tile([P, J], U32, name="xg_codes", align_bytes=64)
+        wg_raw = keep.tile([P, 2 * N], U8, name="wg_raw", tag="late3")
+        nc.sync.dma_start(wg_raw[:].bitcast(I32), wg_words[0].bitcast(I32))
+        xg_codes = keep.tile([P, J], U32, name="xg_codes", tag="pick2", align_bytes=64)
         nc.sync.dma_start(xg_codes[:].bitcast(I32), xg_words[0].rearrange("p j t -> p (j t)").bitcast(I32))
-        wg_codes = keep.tile([P, 2 * N], U8, name="wg_codes", align_bytes=64)
-        nc.sync.dma_start(wg_codes[:].bitcast(I32), wg_words[0].bitcast(I32))
         old_sb = [keep.tile([P, T], F32, name="old0")]
-        nc.sync.dma_start(old_sb[0][:], old_rows[0])
+        nc.sync.dma_start(old_sb[0][:], old_rows[:, 0, :])
 
         in_scales = keep.tile([P, SCALE_BYTES], U8, name="in_scales", align_bytes=64)
         nc.vector.memset(in_scales[:].bitcast(I32), 0)
@@ -60,117 +61,155 @@ def tile_list_head_page_drift_pl_kernel(
                 in_scales[32 * q : 32 * q + 4, :].bitcast(I32), staged[4 * q : 4 * q + 4, :].bitcast(I32)
             )
 
-        pages = [keep.tile([P, T], F32, name="page%d" % i) for i in range(PACK)]
-        for page in pages:
-            nc.vector.memset(page[:], 0.0)
+        pages = [keep.tile([P, T], F32, name="page%d" % t) for t in range(PACK - 1)]
+        for t in range(PACK - 1):
+            (nc.vector if t < 2 else nc.gpsimd).memset(pages[t][:], 0.0)
+        pages.append(pages[1])
         identity = keep.tile([P, P], F32, name="identity")
         make_identity(nc, identity[:])
 
-        wv_codes = keep.tile([P, 2 * N], U8, name="wv_codes", align_bytes=64)
-        nc.vector.tensor_copy(
-            wv_codes[:].bitcast(U16).rearrange("p (t q) -> p t q", t=PACK),
-            wv_raw[:].bitcast(U16).rearrange("p (q t) -> p t q", t=PACK),
-        )
+        def deal_words(engine_copy, raw, name):
+            codes = keep.tile([P, 2 * N], U8, name=name, tag=name, align_bytes=64)
+            engine_copy(
+                codes[:].bitcast(U16).rearrange("p (t q) -> p t q", t=PACK),
+                raw[:].bitcast(U16).rearrange("p (q t) -> p t q", t=PACK),
+            )
+            return codes
+
+        wv_codes = deal_words(nc.vector.tensor_copy, wv_raw, "wv_codes")
 
         xv_bf = keep.tile([P, J, PACK], BF16, name="xv_bf", align_bytes=64)
         nc.vector.tensor_copy(
             xv_bf[:].rearrange("p (c i) t -> p c t i", i=4), xv_raw[:].rearrange("p t (c i) -> p c t i", i=4)
         )
+        wg_codes = deal_words(nc.vector.tensor_copy, wg_raw, "pick3")
         xv_codes = keep.tile([P, J], U32, name="xv_codes", align_bytes=64)
         xv_scale = keep.tile([P, J], U8, name="xv_scale", align_bytes=64)
         nc.vector.quantize_mx(
             out=xv_codes[:].bitcast(E4M3), scales=xv_scale[:], in_=xv_bf[:].rearrange("p j t -> p (j t)")
         )
-        wv_scale = keep.tile([P, N], U8, name="wv_scale", align_bytes=64)
-        nc.vector.tensor_copy(
-            wv_scale[:].rearrange("p (t q) -> p t q", t=PACK),
-            in_scales[:, WV0:SCALE_BYTES].rearrange("p (q t) -> p t q", t=PACK),
-        )
+        w_by_slot = in_scales[:, WG0:XG0].rearrange("p (w q t) -> p t w q", w=2, t=PACK)
+        first_scale = keep.tile([P, 2, P], U8, name="first_scale", tag="pick1", align_bytes=64)
+        nc.vector.tensor_copy(first_scale[:], w_by_slot[:, 0])
+        later_scale = keep.tile([P, PACK - 1, 2, P], U8, name="later_scale", align_bytes=64)
+        nc.vector.tensor_copy(later_scale[:], w_by_slot[:, 1:PACK])
 
         for t in range(1, PACK):
             old_t = keep.tile([P, T], F32, name="old%d" % t, tag="late%d" % t)
-            nc.sync.dma_start(old_t[:], old_rows[t])
+            nc.sync.dma_start(old_t[:], old_rows[:, t, :])
             old_sb.append(old_t)
 
-        g_ps = []
-        for h in range(2):
-            bank = psum.tile([P, N], F32, name="g_ps%d" % h)
+        bank_a = psum.tile([P, J], F32, name="bank_a", tag="sum_t0")
+        bank_b = psum.tile([P, J], F32, name="bank_b", tag="sum_t1")
+        bank_c = psum.tile([P, 2, J], F32, name="bank_c")
+        bank_d = psum.tile([P, 2, J], F32, name="bank_d")
+        bank_e = psum.tile([P, 2, J], F32, name="bank_e")
+        g_ps = [bank_a[:], bank_c[:, 0, :], bank_d[:, 0, :], bank_d[:, 1, :]]
+        v_ps = [bank_b[:], bank_c[:, 1, :], bank_e[:, 0, :], bank_e[:, 1, :]]
+        gates = []
+        for t in range(PACK):
+            w_scale = first_scale if t == 0 else later_scale[:, t - 1]
             nc.tensor.matmul_mx(
-                out=bank[:],
-                lhsT=xg_codes[:, h * P : (h + 1) * P].bitcast(E4M3),
-                lhsT_scale=in_scales[:, XG0 + h * P : XG0 + (h + 1) * P],
-                rhs=wg_codes[:].bitcast(E2M1),
-                rhs_scale=in_scales[:, WG0:XG0],
+                out=g_ps[t],
+                lhsT=wg_codes[:, 2 * P * t : 2 * P * (t + 1)].bitcast(E2M1),
+                lhsT_scale=w_scale[:, 0, :],
+                rhs=xg_codes[:].bitcast(E4M3),
+                rhs_scale=in_scales[:, XG0:SCALE_BYTES],
                 start=True,
                 stop=True,
             )
-            g_ps.append(bank)
-
-        v_ps = []
-        gate_ps = []
-        for u in range(2):
-            v_bank = psum.tile([P, 2, J], F32, name="v_ps%d" % u)
-            for e in range(2):
-                t = 2 * u + e
-                nc.tensor.matmul_mx(
-                    out=v_bank[:, e, :],
-                    lhsT=wv_codes[:, 2 * P * t : 2 * P * (t + 1)].bitcast(E2M1),
-                    lhsT_scale=wv_scale[:, P * t : P * (t + 1)],
-                    rhs=xv_codes[:].bitcast(E4M3),
-                    rhs_scale=xv_scale[:],
-                    start=True,
-                    stop=True,
-                )
-            v_ps.append(v_bank)
-            gate_bank = psum.tile([P, 2, J], F32, name="gate_ps%d" % u)
-            for h in range(2):
-                gate_t = keep.tile([P, 2, P], F32, name="gate_t%d%d" % (u, h))
-                nc.scalar.activation(
-                    gate_t[:], g_ps[h][:].rearrange("j (q t) -> j t q", t=PACK)[:, 2 * u : 2 * u + 2, :], ACT.Sigmoid
-                )
-                for e in range(2):
-                    nc.tensor.transpose(gate_bank[:, e, h * P : (h + 1) * P], gate_t[:, e, :], identity[:])
-            gate_ps.append(gate_bank)
-
-        y = [keep.tile([P, 2, T], F32, name="y%d" % u) for u in range(2)]
-        y_bf = [keep.tile([P, CHUNK, PACK], BF16, name="y_bf%d" % c, align_bytes=64) for c in range(N_CHUNKS)]
-
-        def round_pair(engine_copy, u, c):
-            cols = slice(c * CHUNK, (c + 1) * CHUNK)
-            engine_copy(
-                y_bf[c][:, :, 2 * u : 2 * u + 2].rearrange("p (c i) t -> p c t i", i=4),
-                y[u][:, :, cols].rearrange("p t (c i) -> p c t i", i=4),
+            nc.tensor.matmul_mx(
+                out=v_ps[t],
+                lhsT=wv_codes[:, 2 * P * t : 2 * P * (t + 1)].bitcast(E2M1),
+                lhsT_scale=w_scale[:, 1, :],
+                rhs=xv_codes[:].bitcast(E4M3),
+                rhs_scale=xv_scale[:],
+                start=True,
+                stop=True,
             )
 
+        picked = []
         for t in range(PACK):
-            u, e = divmod(t, 2)
-            picked = keep.tile([P, J], F32, name="picked%d" % t)
-            nc.scalar.activation(picked[:], old_sb[t][:].indirect(offsets[:]), ACT.Copy)
-            diff = keep.tile([P, J], F32, name="diff%d" % t)
-            nc.vector.tensor_tensor(diff[:], v_ps[u][:, e, :], picked[:], ALU.subtract)
-            drift = keep.tile([P, J], F32, name="drift%d" % t)
-            nc.vector.tensor_tensor(drift[:], gate_ps[u][:, e, :], diff[:], ALU.mult)
-            page = pages[t]
-            nc.vector.tensor_copy(page[:].indirect(offsets[:]), drift[:])
-            if t < PACK - 1:
-                nc.gpsimd.tensor_tensor(y[u][:, e, :], old_sb[t][:], page[:], ALU.add)
-                nc.sync.dma_start(out_rows[t], y[u][:, e, :])
-            if t == 1:
-                for c in range(N_CHUNKS):
-                    round_pair(nc.scalar.copy, 0, c)
+            gate = keep.tile([P, J], F32, name="gate%d" % t)
+            nc.scalar.activation(gate[:], g_ps[t], ACT.Sigmoid)
+            gates.append(gate)
+            pick = keep.tile([P, J], F32, name="picked%d" % t, tag="pick%d" % t, align_bytes=64)
+            if t == 0:
+                nc.vector.tensor_copy(pick[:], old_sb[t][:].indirect(offsets[:]))
+            else:
+                nc.scalar.activation(pick[:], old_sb[t][:].indirect(offsets[:]), ACT.Copy)
+            picked.append(pick)
 
-        y_scale = keep.tile([P, T], U8, name="y_scale", align_bytes=64)
-        last = PACK - 1
+        y = [keep.tile([P, 2, T], F32, name="y%d" % u, tag="pick%d" % (u + 2), align_bytes=64) for u in range(2)]
+        y_bf = [keep.tile([P, CHUNK, PACK], BF16, name="y_bf%d" % c, align_bytes=64) for c in range(N_CHUNKS)]
+        diffs = {}
+
+        def subtract(t):
+            diffs[t] = keep.tile([P, J], F32, name="diff%d" % t)
+            nc.vector.tensor_tensor(diffs[t][:], v_ps[t], picked[t][:], ALU.subtract)
+
+        def scatter(t):
+            nc.vector.tensor_tensor(pages[t][:].indirect(offsets[:]), diffs[t][:], gates[t][:], ALU.mult)
+
+        def add(t, cols):
+            nc.vector.tensor_tensor(y[t // 2][:, t % 2, cols], old_sb[t][:, cols], pages[t][:, cols], ALU.add)
+
+        def add_on_tensor(t):
+            for h in range(T // BANK):
+                sum_t = psum.tile([P, PACK, P], F32, name="sum_t", tag="sum_t%d" % h)
+                for k, source in enumerate((old_sb[t], pages[t])):
+                    for b in range(PACK):
+                        c0 = h * BANK + b * P
+                        nc.tensor.matmul(
+                            sum_t[:, b, :],
+                            lhsT=source[:, c0 : c0 + P],
+                            rhs=identity[:],
+                            is_transpose=True,
+                            start=(k == 0 and b == 0),
+                            stop=(k == 1 and b == PACK - 1),
+                        )
+                sum_sb = keep.tile([P, PACK, P], F32, name="sum_sb%d" % h)
+                nc.scalar.copy(sum_sb[:], sum_t[:])
+                back = psum.tile([P, PACK, P], F32, name="back%d" % h)
+                for b in range(PACK):
+                    nc.tensor.transpose(back[:, b, :], sum_sb[:, b, :], identity[:])
+                nc.scalar.copy(y[t // 2][:, t % 2, h * BANK : (h + 1) * BANK], back[:].rearrange("p b c -> p (b c)"))
+            nc.scalar.dma_start(out_rows[:, t, :], y[t // 2][:, t % 2, :])
+
+        def round_pair(engine_copy, u, c, lo, hi):
+            engine_copy(
+                y_bf[c][:, lo:hi, 2 * u : 2 * u + 2].rearrange("p (c i) t -> p c t i", i=4),
+                y[u][:, :, c * CHUNK + lo : c * CHUNK + hi].rearrange("p t (c i) -> p c t i", i=4),
+            )
+
+        subtract(0)
+        scatter(0)
+        add_on_tensor(0)
+        subtract(1)
+        for t in range(1, PACK - 1):
+            scatter(t)
+            subtract(t + 1)
+            add(t, slice(0, T))
+            nc.sync.dma_start(out_rows[:, t, :], y[t // 2][:, t % 2, :])
         for c in range(N_CHUNKS):
-            cols = slice(c * CHUNK, (c + 1) * CHUNK)
-            nc.vector.tensor_tensor(y[1][:, 1, cols], old_sb[last][:, cols], pages[last][:, cols], ALU.add)
+            round_pair(nc.scalar.copy, 0, c, 0, CHUNK)
+        last = PACK - 1
+        scatter(last)
+        for c in range(N_CHUNKS):
+            add(last, slice(c * CHUNK, (c + 1) * CHUNK))
             if c % 2 == 1:
                 half = slice((c - 1) * CHUNK, (c + 1) * CHUNK)
-                nc.sync.dma_start(out_rows[last][:, half], y[1][:, 1, half])
+                nc.sync.dma_start(out_rows[:, last, half], y[1][:, 1, half])
+        round_pair(nc.scalar.copy, 1, 0, 0, CHUNK)
+        round_pair(nc.scalar.copy, 1, 1, 0, CHUNK)
+        round_pair(nc.scalar.copy, 1, 2, 0, CHUNK // 2)
+        round_pair(nc.vector.tensor_copy, 1, 3, 0, CHUNK)
+        round_pair(nc.vector.tensor_copy, 1, 2, CHUNK // 2, CHUNK)
+
+        y_scale = keep.tile([P, T], U8, name="y_scale", align_bytes=64)
         words_out = out_1[0].rearrange("p c t -> p (c t)").bitcast(I32)
         for c in (0, 3, 1, 2):
             cols = slice(c * CHUNK, (c + 1) * CHUNK)
-            round_pair(nc.vector.tensor_copy if c == 3 else nc.scalar.copy, 1, c)
             y_codes = keep.tile([P, CHUNK], U32, name="y_codes%d" % c, align_bytes=64)
             nc.vector.quantize_mx(
                 out=y_codes[:].bitcast(E4M3), scales=y_scale[:, cols], in_=y_bf[c][:].rearrange("p c t -> p (c t)")

@@ -64,7 +64,7 @@ def tile_list_head_page_drift_pl_kernel(
         pages = [keep.tile([P, T], F32, name="page%d" % t) for t in range(PACK - 1)]
         for t in range(PACK - 1):
             (nc.vector if t < 2 else nc.gpsimd).memset(pages[t][:], 0.0)
-        pages.append(pages[1])
+        pages.append(pages[0])
         identity = keep.tile([P, P], F32, name="identity")
         make_identity(nc, identity[:])
 
@@ -99,10 +99,10 @@ def tile_list_head_page_drift_pl_kernel(
             nc.sync.dma_start(old_t[:], old_rows[:, t, :])
             old_sb.append(old_t)
 
-        bank_a = psum.tile([P, J], F32, name="bank_a", tag="sum_t0")
-        bank_b = psum.tile([P, J], F32, name="bank_b", tag="sum_t1")
-        bank_c = psum.tile([P, 2, J], F32, name="bank_c")
-        bank_d = psum.tile([P, 2, J], F32, name="bank_d")
+        bank_a = psum.tile([P, J], F32, name="bank_a", tag="back0")
+        bank_b = psum.tile([P, J], F32, name="bank_b", tag="back1")
+        bank_c = psum.tile([P, 2, J], F32, name="bank_c", tag="bank_c")
+        bank_d = psum.tile([P, 2, J], F32, name="bank_d", tag="bank_d")
         bank_e = psum.tile([P, 2, J], F32, name="bank_e")
         g_ps = [bank_a[:], bank_c[:, 0, :], bank_d[:, 0, :], bank_d[:, 1, :]]
         v_ps = [bank_b[:], bank_c[:, 1, :], bank_e[:, 0, :], bank_e[:, 1, :]]
@@ -140,8 +140,7 @@ def tile_list_head_page_drift_pl_kernel(
                 nc.scalar.activation(pick[:], old_sb[t][:].indirect(offsets[:]), ACT.Copy)
             picked.append(pick)
 
-        y = [keep.tile([P, 2, T], F32, name="y%d" % u, tag="pick%d" % (u + 2), align_bytes=64) for u in range(2)]
-        y_bf = [keep.tile([P, CHUNK, PACK], BF16, name="y_bf%d" % c, align_bytes=64) for c in range(N_CHUNKS)]
+        y = keep.tile([P, PACK, T], F32, name="y")
         diffs = {}
 
         def subtract(t):
@@ -152,7 +151,8 @@ def tile_list_head_page_drift_pl_kernel(
             nc.vector.tensor_tensor(pages[t][:].indirect(offsets[:]), diffs[t][:], gates[t][:], ALU.mult)
 
         def add(t, cols):
-            nc.vector.tensor_tensor(y[t // 2][:, t % 2, cols], old_sb[t][:, cols], pages[t][:, cols], ALU.add)
+            nc.vector.tensor_tensor(y[:, t, cols], old_sb[t][:, cols], pages[t][:, cols], ALU.add)
+
 
         def add_on_tensor(t):
             for h in range(T // BANK):
@@ -168,47 +168,44 @@ def tile_list_head_page_drift_pl_kernel(
                             start=(k == 0 and b == 0),
                             stop=(k == 1 and b == PACK - 1),
                         )
-                sum_sb = keep.tile([P, PACK, P], F32, name="sum_sb%d" % h)
+                sum_sb = keep.tile([P, PACK, P], F32, name="sum_sb%d%d" % (t, h))
                 nc.scalar.copy(sum_sb[:], sum_t[:])
-                back = psum.tile([P, PACK, P], F32, name="back%d" % h)
+                back = psum.tile([P, PACK, P], F32, name="back", tag="back%d" % h)
                 for b in range(PACK):
                     nc.tensor.transpose(back[:, b, :], sum_sb[:, b, :], identity[:])
-                nc.scalar.copy(y[t // 2][:, t % 2, h * BANK : (h + 1) * BANK], back[:].rearrange("p b c -> p (b c)"))
-            nc.scalar.dma_start(out_rows[:, t, :], y[t // 2][:, t % 2, :])
+                nc.scalar.copy(y[:, t, h * BANK : (h + 1) * BANK], back[:].rearrange("p b c -> p (b c)"))
+                if t == 1 or h == 1:
+                    done = slice(h * BANK if t == 1 else 0, (h + 1) * BANK)
+                    nc.scalar.dma_start(out_rows[:, t, done], y[:, t, done])
 
-        def round_pair(engine_copy, u, c, lo, hi):
-            engine_copy(
-                y_bf[c][:, lo:hi, 2 * u : 2 * u + 2].rearrange("p (c i) t -> p c t i", i=4),
-                y[u][:, :, c * CHUNK + lo : c * CHUNK + hi].rearrange("p t (c i) -> p c t i", i=4),
-            )
-
-        subtract(0)
-        scatter(0)
-        add_on_tensor(0)
-        subtract(1)
-        for t in range(1, PACK - 1):
+        for t in range(PACK - 1):
+            subtract(t)
             scatter(t)
-            subtract(t + 1)
-            add(t, slice(0, T))
-            nc.sync.dma_start(out_rows[:, t, :], y[t // 2][:, t % 2, :])
-        for c in range(N_CHUNKS):
-            round_pair(nc.scalar.copy, 0, c, 0, CHUNK)
         last = PACK - 1
+        subtract(last)
+        add(2, slice(0, T))
+        nc.sync.dma_start(out_rows[:, 2, :], y[:, 2, :])
+        for t in range(2):
+            add_on_tensor(t)
         scatter(last)
         for c in range(N_CHUNKS):
             add(last, slice(c * CHUNK, (c + 1) * CHUNK))
             if c % 2 == 1:
                 half = slice((c - 1) * CHUNK, (c + 1) * CHUNK)
-                nc.sync.dma_start(out_rows[:, last, half], y[1][:, 1, half])
-        round_pair(nc.scalar.copy, 1, 0, 0, CHUNK)
-        round_pair(nc.scalar.copy, 1, 1, 0, CHUNK)
-        round_pair(nc.scalar.copy, 1, 2, 0, CHUNK // 2)
-        round_pair(nc.vector.tensor_copy, 1, 3, 0, CHUNK)
-        round_pair(nc.vector.tensor_copy, 1, 2, CHUNK // 2, CHUNK)
+                nc.sync.dma_start(out_rows[:, last, half], y[:, last, half])
+
+        y_bf = {}
+        for c in (0, 2, 1, 3):
+            y_bf[c] = keep.tile([P, CHUNK, PACK], BF16, name="y_bf%d" % c, align_bytes=64)
+            engine_copy = nc.vector.tensor_copy if c >= 2 else nc.scalar.copy
+            engine_copy(
+                y_bf[c][:].rearrange("p (c i) t -> p c t i", i=4),
+                y[:, :, c * CHUNK : (c + 1) * CHUNK].rearrange("p t (c i) -> p c t i", i=4),
+            )
 
         y_scale = keep.tile([P, T], U8, name="y_scale", align_bytes=64)
         words_out = out_1[0].rearrange("p c t -> p (c t)").bitcast(I32)
-        for c in (0, 3, 1, 2):
+        for c in (2, 0, 3, 1):
             cols = slice(c * CHUNK, (c + 1) * CHUNK)
             y_codes = keep.tile([P, CHUNK], U32, name="y_codes%d" % c, align_bytes=64)
             nc.vector.quantize_mx(

@@ -19,9 +19,16 @@ ACT = mybir.ActivationFunctionType
 
 P = 128
 PACK = 4
-BANK = 512
+QUADRANTS = 4
+HALF = 512
+BLOCKS = HALF // P
 CHUNK = 256
-N_CHUNKS = T // CHUNK
+LINE = 4
+TENSOR_SLOTS = (0, 1)
+SCALAR_CHUNKS = (0, 1)
+ROUND_ORDER = (0, 2, 1, 3)
+QUANTISE_ORDER = (2, 0, 3, 1)
+WG0, WV0, XG0, SCALE_BYTES = 0, N, 2 * N, 2 * N + J
 
 
 def tile_list_head_page_drift_pl_kernel(
@@ -37,81 +44,81 @@ def tile_list_head_page_drift_pl_kernel(
 
         offsets = keep.tile([P, J // 16], U16, name="offsets")
 
-        WG0, WV0, XG0, SCALE_BYTES = 0, N, 2 * N, 2 * N + J
-        staged = keep.tile([16, SCALE_BYTES], U8, name="staged", tag="pick0", align_bytes=64)
+        wv_raw = keep.tile([P, 2 * N], U8, name="wv_raw", tag="old0", align_bytes=64)
+        nc.sync.dma_start(wv_raw[:].bitcast(I32), wv_words[0].bitcast(I32))
+        staged = keep.tile([16, SCALE_BYTES], U8, name="staged", tag="picked0", align_bytes=64)
         nc.sync.dma_start(staged[:, WG0:WV0].bitcast(I32), wg_scales[0].bitcast(I32))
         nc.sync.dma_start(staged[:, WV0:XG0].bitcast(I32), wv_scales[0].bitcast(I32))
         nc.sync.dma_start(staged[:, XG0:SCALE_BYTES].bitcast(I32), xg_scales[0].bitcast(I32))
         nc.sync.dma_start(offsets[:], offs)
-        wv_raw = keep.tile([P, 2 * N], U8, name="wv_raw", tag="late1")
-        nc.sync.dma_start(wv_raw[:].bitcast(I32), wv_words[0].bitcast(I32))
-        xv_raw = keep.tile([P, PACK, J], F32, name="xv_raw", tag="late2")
+        xv_raw = keep.tile([P, PACK, J], F32, name="xv_raw", tag="old1", align_bytes=64)
         nc.sync.dma_start(xv_raw[:], xv.rearrange("(p t) j -> p t j", t=PACK))
-        wg_raw = keep.tile([P, 2 * N], U8, name="wg_raw", tag="late3")
+        wg_raw = keep.tile([P, 2 * N], U8, name="wg_raw", tag="old2", align_bytes=64)
         nc.sync.dma_start(wg_raw[:].bitcast(I32), wg_words[0].bitcast(I32))
-        xg_codes = keep.tile([P, J], U32, name="xg_codes", tag="pick2", align_bytes=64)
+        xg_codes = keep.tile([P, J], U32, name="xg_codes", align_bytes=64)
         nc.sync.dma_start(xg_codes[:].bitcast(I32), xg_words[0].rearrange("p j t -> p (j t)").bitcast(I32))
-        old_sb = [keep.tile([P, T], F32, name="old0")]
-        nc.sync.dma_start(old_sb[0][:], old_rows[:, 0, :])
 
         in_scales = keep.tile([P, SCALE_BYTES], U8, name="in_scales", align_bytes=64)
         nc.vector.memset(in_scales[:].bitcast(I32), 0)
-        for q in range(4):
+        for q in range(QUADRANTS):
             nc.scalar.dma_start(
                 in_scales[32 * q : 32 * q + 4, :].bitcast(I32), staged[4 * q : 4 * q + 4, :].bitcast(I32)
             )
 
         pages = [keep.tile([P, T], F32, name="page%d" % t) for t in range(PACK - 1)]
-        for t in range(PACK - 1):
-            (nc.vector if t < 2 else nc.gpsimd).memset(pages[t][:], 0.0)
+        nc.vector.memset(pages[0][:], 0.0)
+        nc.vector.memset(pages[1][:], 0.0)
+        nc.gpsimd.memset(pages[2][:], 0.0)
         pages.append(pages[0])
         identity = keep.tile([P, P], F32, name="identity")
         make_identity(nc, identity[:])
 
-        def deal_words(engine_copy, raw, name):
-            codes = keep.tile([P, 2 * N], U8, name=name, tag=name, align_bytes=64)
-            engine_copy(
+        def deal_words(codes, raw):
+            nc.vector.tensor_copy(
                 codes[:].bitcast(U16).rearrange("p (t q) -> p t q", t=PACK),
                 raw[:].bitcast(U16).rearrange("p (q t) -> p t q", t=PACK),
             )
-            return codes
 
-        wv_codes = deal_words(nc.vector.tensor_copy, wv_raw, "wv_codes")
+        wv_codes = keep.tile([P, 2 * N], U8, name="wv_codes", align_bytes=64)
+        deal_words(wv_codes, wv_raw)
 
-        xv_bf = keep.tile([P, J, PACK], BF16, name="xv_bf", align_bytes=64)
+        xv_bf = keep.tile([P, J, PACK], BF16, name="xv_bf", tag="old3", align_bytes=64)
         nc.vector.tensor_copy(
-            xv_bf[:].rearrange("p (c i) t -> p c t i", i=4), xv_raw[:].rearrange("p t (c i) -> p c t i", i=4)
+            xv_bf[:].rearrange("p (c i) t -> p c t i", i=LINE), xv_raw[:].rearrange("p t (c i) -> p c t i", i=LINE)
         )
-        wg_codes = deal_words(nc.vector.tensor_copy, wg_raw, "pick3")
+        wg_codes = keep.tile([P, 2 * N], U8, name="wg_codes", tag="picked3", align_bytes=64)
+        deal_words(wg_codes, wg_raw)
         xv_codes = keep.tile([P, J], U32, name="xv_codes", align_bytes=64)
         xv_scale = keep.tile([P, J], U8, name="xv_scale", align_bytes=64)
         nc.vector.quantize_mx(
             out=xv_codes[:].bitcast(E4M3), scales=xv_scale[:], in_=xv_bf[:].rearrange("p j t -> p (j t)")
         )
+
         w_by_slot = in_scales[:, WG0:XG0].rearrange("p (w q t) -> p t w q", w=2, t=PACK)
-        first_scale = keep.tile([P, 2, P], U8, name="first_scale", tag="pick1", align_bytes=64)
+        first_scale = keep.tile([P, 2, P], U8, name="first_scale", tag="picked12", align_bytes=64)
         nc.vector.tensor_copy(first_scale[:], w_by_slot[:, 0])
         later_scale = keep.tile([P, PACK - 1, 2, P], U8, name="later_scale", align_bytes=64)
         nc.vector.tensor_copy(later_scale[:], w_by_slot[:, 1:PACK])
 
-        for t in range(1, PACK):
-            old_t = keep.tile([P, T], F32, name="old%d" % t, tag="late%d" % t)
+        old_sb = []
+        for t in range(PACK):
+            old_t = keep.tile([P, T], F32, name="old%d" % t, tag="old%d" % t, align_bytes=64)
             nc.sync.dma_start(old_t[:], old_rows[:, t, :])
             old_sb.append(old_t)
 
-        bank_a = psum.tile([P, J], F32, name="bank_a", tag="back0")
-        bank_b = psum.tile([P, J], F32, name="bank_b", tag="back1")
-        bank_c = psum.tile([P, 2, J], F32, name="bank_c", tag="bank_c")
-        bank_d = psum.tile([P, 2, J], F32, name="bank_d", tag="bank_d")
-        bank_e = psum.tile([P, 2, J], F32, name="bank_e")
-        g_ps = [bank_a[:], bank_c[:, 0, :], bank_d[:, 0, :], bank_d[:, 1, :]]
-        v_ps = [bank_b[:], bank_c[:, 1, :], bank_e[:, 0, :], bank_e[:, 1, :]]
-        gates = []
+        g0_bank = psum.tile([P, J], F32, name="g0_bank", tag="sum0")
+        v0_bank = psum.tile([P, J], F32, name="v0_bank", tag="sum1")
+        g12_bank = psum.tile([P, 2, J], F32, name="g12_bank")
+        v12_bank = psum.tile([P, 2, J], F32, name="v12_bank")
+        gv3_bank = psum.tile([P, 2, J], F32, name="gv3_bank")
+        g_ps = [g0_bank[:], g12_bank[:, 0, :], g12_bank[:, 1, :], gv3_bank[:, 0, :]]
+        v_ps = [v0_bank[:], v12_bank[:, 0, :], v12_bank[:, 1, :], gv3_bank[:, 1, :]]
         for t in range(PACK):
             w_scale = first_scale if t == 0 else later_scale[:, t - 1]
+            slot_bytes = slice(2 * P * t, 2 * P * (t + 1))
             nc.tensor.matmul_mx(
                 out=g_ps[t],
-                lhsT=wg_codes[:, 2 * P * t : 2 * P * (t + 1)].bitcast(E2M1),
+                lhsT=wg_codes[:, slot_bytes].bitcast(E2M1),
                 lhsT_scale=w_scale[:, 0, :],
                 rhs=xg_codes[:].bitcast(E4M3),
                 rhs_scale=in_scales[:, XG0:SCALE_BYTES],
@@ -120,7 +127,7 @@ def tile_list_head_page_drift_pl_kernel(
             )
             nc.tensor.matmul_mx(
                 out=v_ps[t],
-                lhsT=wv_codes[:, 2 * P * t : 2 * P * (t + 1)].bitcast(E2M1),
+                lhsT=wv_codes[:, slot_bytes].bitcast(E2M1),
                 lhsT_scale=w_scale[:, 1, :],
                 rhs=xv_codes[:].bitcast(E4M3),
                 rhs_scale=xv_scale[:],
@@ -128,91 +135,93 @@ def tile_list_head_page_drift_pl_kernel(
                 stop=True,
             )
 
-        picked = []
-        for t in range(PACK):
-            gate = keep.tile([P, J], F32, name="gate%d" % t)
-            nc.scalar.activation(gate[:], g_ps[t], ACT.Sigmoid)
-            gates.append(gate)
-            pick = keep.tile([P, J], F32, name="picked%d" % t, tag="pick%d" % t, align_bytes=64)
-            if t == 0:
-                nc.vector.tensor_copy(pick[:], old_sb[t][:].indirect(offsets[:]))
-            else:
-                nc.scalar.activation(pick[:], old_sb[t][:].indirect(offsets[:]), ACT.Copy)
-            picked.append(pick)
+        gate0 = keep.tile([P, J], F32, name="gate0")
+        gate12 = keep.tile([P, 2, J], F32, name="gate12")
+        gate3 = keep.tile([P, J], F32, name="gate3")
+        picked0 = keep.tile([P, J], F32, name="picked0", tag="picked0", align_bytes=64)
+        picked12 = keep.tile([P, 2, J], F32, name="picked12", tag="picked12", align_bytes=64)
+        picked3 = keep.tile([P, J], F32, name="picked3", tag="picked3", align_bytes=64)
+        nc.scalar.activation(gate0[:], g0_bank[:], ACT.Sigmoid)
+        nc.vector.tensor_copy(picked0[:], old_sb[0][:].indirect(offsets[:]))
+        nc.scalar.activation(gate12[:], g12_bank[:], ACT.Sigmoid)
+        nc.scalar.activation(picked12[:, 0, :], old_sb[1][:].indirect(offsets[:]), ACT.Copy)
+        nc.scalar.activation(gate3[:], g_ps[3], ACT.Sigmoid)
+        nc.scalar.activation(picked12[:, 1, :], old_sb[2][:].indirect(offsets[:]), ACT.Copy)
+        nc.scalar.activation(picked3[:], old_sb[3][:].indirect(offsets[:]), ACT.Copy)
+        gates = [gate0[:], gate12[:, 0, :], gate12[:, 1, :], gate3[:]]
 
         y = keep.tile([P, PACK, T], F32, name="y")
-        diffs = {}
-
-        def subtract(t):
-            diffs[t] = keep.tile([P, J], F32, name="diff%d" % t)
-            nc.vector.tensor_tensor(diffs[t][:], v_ps[t], picked[t][:], ALU.subtract)
+        diff0 = keep.tile([P, J], F32, name="diff0")
+        diff12 = keep.tile([P, 2, J], F32, name="diff12")
+        diff3 = keep.tile([P, J], F32, name="diff3")
+        diffs = [diff0[:], diff12[:, 0, :], diff12[:, 1, :], diff3[:]]
 
         def scatter(t):
-            nc.vector.tensor_tensor(pages[t][:].indirect(offsets[:]), diffs[t][:], gates[t][:], ALU.mult)
+            nc.vector.tensor_tensor(pages[t][:].indirect(offsets[:]), diffs[t], gates[t], ALU.mult)
 
-        def add(t, cols):
+        def add_on_vector(t, cols):
             nc.vector.tensor_tensor(y[:, t, cols], old_sb[t][:, cols], pages[t][:, cols], ALU.add)
 
-
         def add_on_tensor(t):
-            for h in range(T // BANK):
-                sum_t = psum.tile([P, PACK, P], F32, name="sum_t", tag="sum_t%d" % h)
+            for h in range(T // HALF):
+                sum_t = psum.tile([P, BLOCKS, P], F32, name="sum_t", tag="sum%d" % h)
                 for k, source in enumerate((old_sb[t], pages[t])):
-                    for b in range(PACK):
-                        c0 = h * BANK + b * P
+                    for b in range(BLOCKS):
+                        c0 = h * HALF + b * P
                         nc.tensor.matmul(
                             sum_t[:, b, :],
                             lhsT=source[:, c0 : c0 + P],
                             rhs=identity[:],
                             is_transpose=True,
                             start=(k == 0 and b == 0),
-                            stop=(k == 1 and b == PACK - 1),
+                            stop=(k == 1 and b == BLOCKS - 1),
                         )
-                sum_sb = keep.tile([P, PACK, P], F32, name="sum_sb%d%d" % (t, h))
+                sum_sb = keep.tile([P, BLOCKS, P], F32, name="sum_sb%d%d" % (t, h))
                 nc.scalar.copy(sum_sb[:], sum_t[:])
-                back = psum.tile([P, PACK, P], F32, name="back", tag="back%d" % h)
-                for b in range(PACK):
+                back = psum.tile([P, BLOCKS, P], F32, name="back", tag="back%d" % h)
+                for b in range(BLOCKS):
                     nc.tensor.transpose(back[:, b, :], sum_sb[:, b, :], identity[:])
-                nc.scalar.copy(y[:, t, h * BANK : (h + 1) * BANK], back[:].rearrange("p b c -> p (b c)"))
+                nc.scalar.copy(y[:, t, h * HALF : (h + 1) * HALF], back[:].rearrange("p b c -> p (b c)"))
                 if t == 1 or h == 1:
-                    done = slice(h * BANK if t == 1 else 0, (h + 1) * BANK)
+                    done = slice(h * HALF if t == 1 else 0, (h + 1) * HALF)
                     nc.scalar.dma_start(out_rows[:, t, done], y[:, t, done])
 
-        for t in range(PACK - 1):
-            subtract(t)
-            scatter(t)
-        last = PACK - 1
-        subtract(last)
-        add(2, slice(0, T))
+        nc.vector.tensor_tensor(diff0[:], v0_bank[:], picked0[:], ALU.subtract)
+        scatter(0)
+        nc.vector.tensor_tensor(diff12[:], v12_bank[:], picked12[:], ALU.subtract)
+        scatter(1)
+        nc.vector.tensor_tensor(diff3[:], v_ps[3], picked3[:], ALU.subtract)
+        scatter(2)
+        add_on_vector(2, slice(0, T))
         nc.sync.dma_start(out_rows[:, 2, :], y[:, 2, :])
-        for t in range(2):
+        for t in TENSOR_SLOTS:
             add_on_tensor(t)
-        scatter(last)
-        for c in range(N_CHUNKS):
-            add(last, slice(c * CHUNK, (c + 1) * CHUNK))
-            if c % 2 == 1:
-                half = slice((c - 1) * CHUNK, (c + 1) * CHUNK)
-                nc.sync.dma_start(out_rows[:, last, half], y[:, last, half])
+        scatter(3)
+        for h in range(T // HALF):
+            for c0 in range(h * HALF, (h + 1) * HALF, CHUNK):
+                add_on_vector(3, slice(c0, c0 + CHUNK))
+            half = slice(h * HALF, (h + 1) * HALF)
+            nc.sync.dma_start(out_rows[:, 3, half], y[:, 3, half])
 
         y_bf = {}
-        for c in (0, 2, 1, 3):
+        for c in ROUND_ORDER:
             y_bf[c] = keep.tile([P, CHUNK, PACK], BF16, name="y_bf%d" % c, align_bytes=64)
-            engine_copy = nc.vector.tensor_copy if c >= 2 else nc.scalar.copy
+            engine_copy = nc.scalar.copy if c in SCALAR_CHUNKS else nc.vector.tensor_copy
             engine_copy(
-                y_bf[c][:].rearrange("p (c i) t -> p c t i", i=4),
-                y[:, :, c * CHUNK : (c + 1) * CHUNK].rearrange("p t (c i) -> p c t i", i=4),
+                y_bf[c][:].rearrange("p (c i) t -> p c t i", i=LINE),
+                y[:, :, c * CHUNK : (c + 1) * CHUNK].rearrange("p t (c i) -> p c t i", i=LINE),
             )
 
         y_scale = keep.tile([P, T], U8, name="y_scale", align_bytes=64)
         words_out = out_1[0].rearrange("p c t -> p (c t)").bitcast(I32)
-        for c in (2, 0, 3, 1):
+        for c in QUANTISE_ORDER:
             cols = slice(c * CHUNK, (c + 1) * CHUNK)
             y_codes = keep.tile([P, CHUNK], U32, name="y_codes%d" % c, align_bytes=64)
             nc.vector.quantize_mx(
                 out=y_codes[:].bitcast(E4M3), scales=y_scale[:, cols], in_=y_bf[c][:].rearrange("p c t -> p (c t)")
             )
             nc.sync.dma_start(words_out[:, cols], y_codes[:].bitcast(I32))
-        for q in range(4):
+        for q in range(QUADRANTS):
             queue = nc.sync if q % 2 else nc.scalar
             queue.dma_start(
                 out_2[0, 4 * q : 4 * q + 4, :].bitcast(I32), y_scale[32 * q : 32 * q + 4, :].bitcast(I32)

from contextlib import ExitStack

import concourse.mybir as mybir
from concourse.masks import make_identity

K, T, J, N, L = 512, 1024, 256, 512, 512
FLOPS = 2 * K * N * J + 2 * L * N * J

F32 = mybir.dt.float32
BF16 = mybir.dt.bfloat16
I32 = mybir.dt.int32
U32 = mybir.dt.uint32
U16 = mybir.dt.uint16
U8 = mybir.dt.uint8
E4M3 = mybir.dt.float8_e4m3fn_x4
E2M1 = mybir.dt.float4_e2m1fn_x4
ALU = mybir.AluOpType
ACT = mybir.ActivationFunctionType

P = 128
PACK = 4
QUADRANTS = 4
HALF = 512
BLOCKS = HALF // P
CHUNK = 256
LINE = 4
TENSOR_SLOTS = (0, 1)
SCALAR_CHUNKS = (0, 1)
ROUND_ORDER = (0, 2, 1, 3)
QUANTISE_ORDER = (2, 0, 3, 1)
WG0, WV0, XG0, SCALE_BYTES = 0, N, 2 * N, 2 * N + J


def tile_list_head_page_drift_pl_kernel(
    tc, xv, wv_words, wv_scales, xg_words, xg_scales, wg_words, wg_scales, old, offs, out_0, out_1, out_2
):
    nc = tc.nc
    old_rows = old.rearrange("(p t) c -> p t c", t=PACK)
    out_rows = out_0.rearrange("(p t) c -> p t c", t=PACK)

    with ExitStack() as ctx:
        keep = ctx.enter_context(tc.tile_pool(name="keep", bufs=1))
        psum = ctx.enter_context(tc.psum_pool(name="psum", bufs=1))

        offsets = keep.tile([P, J // 16], U16, name="offsets")

        wv_raw = keep.tile([P, 2 * N], U8, name="wv_raw", tag="old0", align_bytes=64)
        nc.sync.dma_start(wv_raw[:].bitcast(I32), wv_words[0].bitcast(I32))
        staged = keep.tile([16, SCALE_BYTES], U8, name="staged", tag="picked0", align_bytes=64)
        nc.sync.dma_start(staged[:, WG0:WV0].bitcast(I32), wg_scales[0].bitcast(I32))
        nc.sync.dma_start(staged[:, WV0:XG0].bitcast(I32), wv_scales[0].bitcast(I32))
        nc.sync.dma_start(staged[:, XG0:SCALE_BYTES].bitcast(I32), xg_scales[0].bitcast(I32))
        nc.sync.dma_start(offsets[:], offs)
        xv_raw = keep.tile([P, PACK, J], F32, name="xv_raw", tag="old1", align_bytes=64)
        nc.sync.dma_start(xv_raw[:], xv.rearrange("(p t) j -> p t j", t=PACK))
        wg_raw = keep.tile([P, 2 * N], U8, name="wg_raw", tag="old2", align_bytes=64)
        nc.sync.dma_start(wg_raw[:].bitcast(I32), wg_words[0].bitcast(I32))
        xg_codes = keep.tile([P, J], U32, name="xg_codes", align_bytes=64)
        nc.sync.dma_start(xg_codes[:].bitcast(I32), xg_words[0].rearrange("p j t -> p (j t)").bitcast(I32))

        in_scales = keep.tile([P, SCALE_BYTES], U8, name="in_scales", align_bytes=64)
        nc.vector.memset(in_scales[:].bitcast(I32), 0)
        for q in range(QUADRANTS):
            nc.scalar.dma_start(
                in_scales[32 * q : 32 * q + 4, :].bitcast(I32), staged[4 * q : 4 * q + 4, :].bitcast(I32)
            )

        pages = [keep.tile([P, T], F32, name="page%d" % t) for t in range(PACK - 1)]
        nc.vector.memset(pages[0][:], 0.0)
        nc.vector.memset(pages[1][:], 0.0)
        nc.gpsimd.memset(pages[2][:], 0.0)
        pages.append(pages[0])
        identity = keep.tile([P, P], F32, name="identity")
        make_identity(nc, identity[:])

        def deal_words(codes, raw):
            nc.vector.tensor_copy(
                codes[:].bitcast(U16).rearrange("p (t q) -> p t q", t=PACK),
                raw[:].bitcast(U16).rearrange("p (q t) -> p t q", t=PACK),
            )

        wv_codes = keep.tile([P, 2 * N], U8, name="wv_codes", align_bytes=64)
        deal_words(wv_codes, wv_raw)

        xv_bf = keep.tile([P, J, PACK], BF16, name="xv_bf", tag="old3", align_bytes=64)
        nc.vector.tensor_copy(
            xv_bf[:].rearrange("p (c i) t -> p c t i", i=LINE), xv_raw[:].rearrange("p t (c i) -> p c t i", i=LINE)
        )
        wg_codes = keep.tile([P, 2 * N], U8, name="wg_codes", tag="picked3", align_bytes=64)
        deal_words(wg_codes, wg_raw)
        xv_codes = keep.tile([P, J], U32, name="xv_codes", align_bytes=64)
        xv_scale = keep.tile([P, J], U8, name="xv_scale", align_bytes=64)
        nc.vector.quantize_mx(
            out=xv_codes[:].bitcast(E4M3), scales=xv_scale[:], in_=xv_bf[:].rearrange("p j t -> p (j t)")
        )

        w_by_slot = in_scales[:, WG0:XG0].rearrange("p (w q t) -> p t w q", w=2, t=PACK)
        first_scale = keep.tile([P, 2, P], U8, name="first_scale", tag="picked12", align_bytes=64)
        nc.vector.tensor_copy(first_scale[:], w_by_slot[:, 0])
        later_scale = keep.tile([P, PACK - 1, 2, P], U8, name="later_scale", align_bytes=64)
        nc.vector.tensor_copy(later_scale[:], w_by_slot[:, 1:PACK])

        old_sb = []
        for t in range(PACK):
            old_t = keep.tile([P, T], F32, name="old%d" % t, tag="old%d" % t, align_bytes=64)
            nc.sync.dma_start(old_t[:], old_rows[:, t, :])
            old_sb.append(old_t)

        g0_bank = psum.tile([P, J], F32, name="g0_bank", tag="sum0")
        v0_bank = psum.tile([P, J], F32, name="v0_bank", tag="sum1")
        g12_bank = psum.tile([P, 2, J], F32, name="g12_bank")
        v12_bank = psum.tile([P, 2, J], F32, name="v12_bank")
        gv3_bank = psum.tile([P, 2, J], F32, name="gv3_bank")
        g_ps = [g0_bank[:], g12_bank[:, 0, :], g12_bank[:, 1, :], gv3_bank[:, 0, :]]
        v_ps = [v0_bank[:], v12_bank[:, 0, :], v12_bank[:, 1, :], gv3_bank[:, 1, :]]
        for t in range(PACK):
            w_scale = first_scale if t == 0 else later_scale[:, t - 1]
            slot_bytes = slice(2 * P * t, 2 * P * (t + 1))
            nc.tensor.matmul_mx(
                out=g_ps[t],
                lhsT=wg_codes[:, slot_bytes].bitcast(E2M1),
                lhsT_scale=w_scale[:, 0, :],
                rhs=xg_codes[:].bitcast(E4M3),
                rhs_scale=in_scales[:, XG0:SCALE_BYTES],
                start=True,
                stop=True,
            )
            nc.tensor.matmul_mx(
                out=v_ps[t],
                lhsT=wv_codes[:, slot_bytes].bitcast(E2M1),
                lhsT_scale=w_scale[:, 1, :],
                rhs=xv_codes[:].bitcast(E4M3),
                rhs_scale=xv_scale[:],
                start=True,
                stop=True,
            )

        gate0 = keep.tile([P, J], F32, name="gate0")
        gate12 = keep.tile([P, 2, J], F32, name="gate12")
        gate3 = keep.tile([P, J], F32, name="gate3")
        picked0 = keep.tile([P, J], F32, name="picked0", tag="picked0", align_bytes=64)
        picked12 = keep.tile([P, 2, J], F32, name="picked12", tag="picked12", align_bytes=64)
        picked3 = keep.tile([P, J], F32, name="picked3", tag="picked3", align_bytes=64)
        nc.scalar.activation(gate0[:], g0_bank[:], ACT.Sigmoid)
        nc.vector.tensor_copy(picked0[:], old_sb[0][:].indirect(offsets[:]))
        nc.scalar.activation(gate12[:], g12_bank[:], ACT.Sigmoid)
        nc.scalar.activation(picked12[:, 0, :], old_sb[1][:].indirect(offsets[:]), ACT.Copy)
        nc.scalar.activation(gate3[:], g_ps[3], ACT.Sigmoid)
        nc.scalar.activation(picked12[:, 1, :], old_sb[2][:].indirect(offsets[:]), ACT.Copy)
        nc.scalar.activation(picked3[:], old_sb[3][:].indirect(offsets[:]), ACT.Copy)
        gates = [gate0[:], gate12[:, 0, :], gate12[:, 1, :], gate3[:]]

        y = keep.tile([P, PACK, T], F32, name="y")
        diff0 = keep.tile([P, J], F32, name="diff0")
        diff12 = keep.tile([P, 2, J], F32, name="diff12")
        diff3 = keep.tile([P, J], F32, name="diff3")
        diffs = [diff0[:], diff12[:, 0, :], diff12[:, 1, :], diff3[:]]

        def scatter(t):
            nc.vector.tensor_tensor(pages[t][:].indirect(offsets[:]), diffs[t], gates[t], ALU.mult)

        def add_on_vector(t, cols):
            nc.vector.tensor_tensor(y[:, t, cols], old_sb[t][:, cols], pages[t][:, cols], ALU.add)

        def add_on_tensor(t):
            for h in range(T // HALF):
                sum_t = psum.tile([P, BLOCKS, P], F32, name="sum_t", tag="sum%d" % h)
                for k, source in enumerate((old_sb[t], pages[t])):
                    for b in range(BLOCKS):
                        c0 = h * HALF + b * P
                        nc.tensor.matmul(
                            sum_t[:, b, :],
                            lhsT=source[:, c0 : c0 + P],
                            rhs=identity[:],
                            is_transpose=True,
                            start=(k == 0 and b == 0),
                            stop=(k == 1 and b == BLOCKS - 1),
                        )
                sum_sb = keep.tile([P, BLOCKS, P], F32, name="sum_sb%d%d" % (t, h))
                nc.scalar.copy(sum_sb[:], sum_t[:])
                back = psum.tile([P, BLOCKS, P], F32, name="back", tag="back%d" % h)
                for b in range(BLOCKS):
                    nc.tensor.transpose(back[:, b, :], sum_sb[:, b, :], identity[:])
                nc.scalar.copy(y[:, t, h * HALF : (h + 1) * HALF], back[:].rearrange("p b c -> p (b c)"))
                if t == 1 or h == 1:
                    done = slice(h * HALF if t == 1 else 0, (h + 1) * HALF)
                    nc.scalar.dma_start(out_rows[:, t, done], y[:, t, done])

        nc.vector.tensor_tensor(diff0[:], v0_bank[:], picked0[:], ALU.subtract)
        scatter(0)
        nc.vector.tensor_tensor(diff12[:], v12_bank[:], picked12[:], ALU.subtract)
        scatter(1)
        nc.vector.tensor_tensor(diff3[:], v_ps[3], picked3[:], ALU.subtract)
        scatter(2)
        add_on_vector(2, slice(0, T))
        nc.sync.dma_start(out_rows[:, 2, :], y[:, 2, :])
        for t in TENSOR_SLOTS:
            add_on_tensor(t)
        scatter(3)
        for h in range(T // HALF):
            for c0 in range(h * HALF, (h + 1) * HALF, CHUNK):
                add_on_vector(3, slice(c0, c0 + CHUNK))
            half = slice(h * HALF, (h + 1) * HALF)
            nc.sync.dma_start(out_rows[:, 3, half], y[:, 3, half])

        y_bf = {}
        for c in ROUND_ORDER:
            y_bf[c] = keep.tile([P, CHUNK, PACK], BF16, name="y_bf%d" % c, align_bytes=64)
            engine_copy = nc.scalar.copy if c in SCALAR_CHUNKS else nc.vector.tensor_copy
            engine_copy(
                y_bf[c][:].rearrange("p (c i) t -> p c t i", i=LINE),
                y[:, :, c * CHUNK : (c + 1) * CHUNK].rearrange("p t (c i) -> p c t i", i=LINE),
            )

        y_scale = keep.tile([P, T], U8, name="y_scale", align_bytes=64)
        words_out = out_1[0].rearrange("p c t -> p (c t)").bitcast(I32)
        for c in QUANTISE_ORDER:
            cols = slice(c * CHUNK, (c + 1) * CHUNK)
            y_codes = keep.tile([P, CHUNK], U32, name="y_codes%d" % c, align_bytes=64)
            nc.vector.quantize_mx(
                out=y_codes[:].bitcast(E4M3), scales=y_scale[:, cols], in_=y_bf[c][:].rearrange("p c t -> p (c t)")
            )
            nc.sync.dma_start(words_out[:, cols], y_codes[:].bitcast(I32))
        for q in range(QUADRANTS):
            queue = nc.sync if q % 2 else nc.scalar
            queue.dma_start(
                out_2[0, 4 * q : 4 * q + 4, :].bitcast(I32), y_scale[32 * q : 32 * q + 4, :].bitcast(I32)
            )
